import numpy as np
import ml_dtypes


def mxq(x, axis, fmt="e4m3"):
    dtype, down = {"e4m3": (ml_dtypes.float8_e4m3fn, 7), "e5m2": (ml_dtypes.float8_e5m2, 14)}[fmt]
    v = np.moveaxis(np.asarray(x, np.float32).astype(ml_dtypes.bfloat16).astype(np.float64), axis, -1)
    blocks = v.reshape(v.shape[:-1] + (-1, 32))
    amax = np.abs(blocks).max(-1, keepdims=True)
    byte = np.maximum(np.where(amax > 0, np.frexp(amax)[1] - 1 + 127, 0) - down, 1)
    scale = np.exp2(byte - 127.0)
    codes = (blocks / scale).astype(np.float32).astype(dtype).astype(np.float64)
    return np.moveaxis((codes * scale).reshape(v.shape), -1, axis)


WIDE = False


def mx_kscale(k):
    if not WIDE:
        return np.ones(k)
    levels = np.array([10, -10, 5, -5, 0])
    if k % 512:
        return np.exp2(np.random.permutation(np.resize(levels, k // 32))).repeat(32)
    a = np.empty((k // 512, 16))
    for p in range(k // 512):
        a[p, :8] = np.random.permutation(np.resize(levels, 8))
        for g in range(8):
            far = levels[np.abs(levels - a[p, g]) >= 10]
            a[p, g + 8] = far[np.random.randint(len(far))]
    return np.exp2(a.ravel()).repeat(32)


def f64(x):
    return np.asarray(x).astype(np.float64)


def striped(idx):
    return np.tile(idx.reshape(-1, 16).T, (8, 1)).astype(np.uint16)


def unstriped(offs):
    return offs[:16].T.reshape(-1).astype(np.int64)


def striped8(idx):
    return np.concatenate([x.reshape(-1, 16).T for x in idx]).astype(np.uint16)


def runs(offs, k):
    lists = np.stack([offs[16 * r : 16 * r + 16].T.reshape(-1) for r in range(8)]).astype(np.int64)
    return lists[np.arange(k) % 512 // 64]


def pack_weight(w):
    k, n = w.shape
    w = f64(np.asarray(w, np.float32).astype(ml_dtypes.bfloat16)).reshape(k // 32, 32, n)
    amax = np.abs(w).max(1)
    byte = np.clip(np.where(amax > 0, np.frexp(amax)[1] - 1 + 127 - 7, 1), 1, 254)
    scaled = (w * np.exp2(127.0 - byte)[:, None, :]).reshape(k, n).astype(np.float32)
    words = np.ascontiguousarray(scaled.reshape(k // 512, 128, 4, n).transpose(0, 1, 3, 2)).astype(ml_dtypes.float8_e4m3fn).view(np.uint8)
    return words, np.ascontiguousarray(byte.astype(np.uint8).reshape(k // 512, 16, n))


def unpack_weight(words, scales):
    g, p, n, _ = words.shape
    vals = np.ascontiguousarray(words).view(ml_dtypes.float8_e4m3fn).astype(np.float64) * np.repeat(np.exp2(scales.astype(np.float64) - 127.0), 8, axis=1)[..., None]
    return vals.transpose(0, 1, 3, 2).reshape(g * 512, n)


def relu(v):
    return np.maximum(v, 0.0)


def sigmoid(v):
    return 1.0 / (1.0 + np.exp(-np.maximum(v, -700.0)))

def planes(y):
    n, m = y.shape
    v = y.astype(np.float32).astype(ml_dtypes.bfloat16).astype(np.float64).reshape(n // 32, 32, m)
    top = np.abs(v).max(1)
    byte = np.clip(np.where(top > 0, np.frexp(top)[1] - 1 + 127 - 7, 1), 1, 254)
    codes = (v * np.exp2(127.0 - byte)[:, None, :]).reshape(n, m).astype(np.float32).astype(ml_dtypes.float8_e4m3fn).view(np.uint8)
    words = codes.reshape(n // 512, 128, 4, m).transpose(0, 1, 3, 2)
    return np.ascontiguousarray(words), np.ascontiguousarray(byte.astype(np.uint8).reshape(n // 512, 16, m))


K, T, S, N, G, H = 512, 1024, 512, 512, 2048, 512


def setup_inputs():
    n = np.random.standard_normal
    s = mx_kscale(K)[:, None]
    u = mx_kscale(S)
    packed_xT = pack_weight(n((K, T)) * s)
    packed_dT = pack_weight(n((K, G)) / s)
    packed_w1 = pack_weight(n((H, N)) / np.sqrt(2 * H) / u[:, None])
    packed_w2 = pack_weight(n((H, N)) / np.sqrt(2 * H) / u[:, None])
    return {
        "x_words": packed_xT[0],
        "x_scales": packed_xT[1],
        "d_words": packed_dT[0],
        "d_scales": packed_dT[1],
        "gn": (np.random.uniform(0.5, 1.5, (H, 1)) * u[:, None]).astype(np.float32),
        "gm": (np.random.uniform(0.5, 1.5, (H, 1)) * u[:, None]).astype(np.float32),
        "w1_words": packed_w1[0],
        "w1_scales": packed_w1[1],
        "w2_words": packed_w2[0],
        "w2_scales": packed_w2[1],
        "offs": striped(np.random.permutation(T)[:S]),
        "k1": striped8(np.random.randint(0, G, (8, H))),
        "two": striped(np.random.permutation(T)[:S]),
        "n1": striped8(np.stack([np.random.permutation(S) for _ in range(8)])),
        "n2": striped8(np.stack([np.random.permutation(S) for _ in range(8)])),
        "n3": striped8(np.stack([np.random.permutation(S) for _ in range(8)])),
        "n4": striped8(np.stack([np.random.permutation(S) for _ in range(8)])),
        "n5": striped(np.random.permutation(S)),
        "n6": striped(np.random.permutation(S)),
        "n7": striped(np.random.permutation(S)),
    }


def reference(x_words, x_scales, d_words, d_scales, gn, gm, w1_words, w1_scales, w2_words, w2_scales, offs, k1, two, n1, n2, n3, n4, n5, n6, n7):
    d_k1 = unpack_weight(d_words, d_scales)[np.arange(K)[:, None], runs(k1, K)]
    xq = unpack_weight(x_words, x_scales)[:, unstriped(offs)]
    a = 0.0625 * (d_k1.T @ xq)
    z = f64(gn) * (relu(a - (a[np.arange(H)[:, None], runs(n1, H)])) + 0.5 * (relu(a[np.arange(H)[:, None], runs(n2, H)] - a)))
    x_two = unpack_weight(x_words, x_scales)[:, unstriped(two)]
    b = 0.0625 * (d_k1.T @ x_two)
    st = b[np.arange(H)[:, None], runs(n3, H)] - b
    z2 = f64(gm) * (b * (sigmoid(st[np.arange(H)[:, None], runs(n4, H)])))
    h = unpack_weight(w1_words, w1_scales).T @ mxq(z, 0, "e4m3") + unpack_weight(w2_words, w2_scales).T @ mxq(z2, 0, "e4m3")
    out_0 = np.maximum(h, h[:, unstriped(n5)]) - (np.maximum(h[:, unstriped(n6)], h[:, unstriped(n7)]))
    return (out_0,) + planes(out_0)

@@ -1,0 +1,321 @@
+from contextlib import ExitStack
+
+import concourse.mybir as mybir
+
+F32 = mybir.dt.float32
+BF16 = mybir.dt.bfloat16
+I32 = mybir.dt.int32
+U32 = mybir.dt.uint32
+U16 = mybir.dt.uint16
+U8 = mybir.dt.uint8
+FP8X4 = mybir.dt.float8_e4m3fn_x4
+ALU = mybir.AluOpType
+ACT = mybir.ActivationFunctionType
+
+P = 128
+PACK = 4
+S = 512
+T = 1024
+G = 2048
+SCORE_SCALE = 0.0625
+FLOPS = 4 * 2 * 512 * 512 * 512
+HALVES = [(0, 256), (256, 512)]
+OUT_CHUNKS = [(0, 256), (256, 384), (384, 512)]
+
+
+def words_of(dram):
+    return dram[0].rearrange("p n t -> p (n t)").bitcast(I32)
+
+
+def entries(lst, lo, hi):
+    return lst[:, lo // 16 : hi // 16]
+
+
+def line_walk_rows(ap):
+    return ap.rearrange("p t (c i) -> p c t i", i=4)
+
+
+def line_walk_words(ap):
+    return ap.rearrange("p (c i) t -> p c t i", i=4)
+
+
+def tile_picked_kjhingehopdmix_none_po_kernel(
+    tc, x_words, x_scales, d_words, d_scales, gn, gm, w1_words, w1_scales, w2_words, w2_scales,
+    offs, k1, two, n1, n2, n3, n4, n5, n6, n7, out_0, out_1, out_2,
+):
+    nc = tc.nc
+    with ExitStack() as ctx:
+        lists = ctx.enter_context(tc.tile_pool(name="lists", bufs=1))
+        keep = ctx.enter_context(tc.tile_pool(name="keep", bufs=1))
+        psum = ctx.enter_context(tc.psum_pool(name="psum", bufs=1))
+
+        def load_list(dram, name):
+            lst = lists.tile([P, S // 16], U16, name=name)
+            nc.sync.dma_start(lst[:], dram)
+            return lst
+
+        def sb(shape, dtype, name, over=None):
+            return keep.tile(shape, dtype, name=name, tag=over or name, align_bytes=64)
+
+        k1_l = load_list(k1, "k1_l")
+        d_scale_table = sb([P, G], U8, "d_scale_table")
+        nc.sync.dma_start(
+            d_scale_table[:].bitcast(I32),
+            d_scales[0].bitcast(I32).unsqueeze(1).to_broadcast([16, 8, G // 4]),
+        )
+        x_word_table = sb([P, T], U32, "x_word_table")
+        nc.sync.dma_start(x_word_table[:].bitcast(I32), words_of(x_words))
+        offs_l = load_list(offs, "offs_l")
+        x_scale_table = sb([P, T], U8, "x_scale_table")
+        for q in range(4):
+            nc.sync.dma_start(
+                x_scale_table[:].bitcast(I32)[32 * q : 32 * q + 32, :],
+                x_scales[0].bitcast(I32)[4 * q : 4 * q + 4, :].unsqueeze(0).to_broadcast([8, 4, T // 4]),
+            )
+        d_word_table = sb([P, G], U32, "d_word_table")
+        nc.sync.dma_start(d_word_table[:].bitcast(I32), words_of(d_words))
+        two_l = load_list(two, "two_l")
+        key_scales = sb([P, S], U8, "key_scales")
+        nc.gpsimd.memset(key_scales[:].bitcast(I32), 0)
+        w_scale_raw = sb([P, S], U8, "w_scale_raw")
+        nc.gpsimd.memset(w_scale_raw[:].bitcast(I32), 0)
+        a_win = [sb([P, 2 * S], F32, "a_win%d" % t) for t in range(PACK)]
+        nc.gpsimd.memset(a_win[0][:, S:], 0.0)
+
+        key_scales_picked = sb([P, S], U8, "key_scales_picked")
+        nc.vector.tensor_copy(key_scales_picked[:], d_scale_table[:].indirect(k1_l[:]))
+        key_scales_dealt = sb([P, PACK, P], U8, "key_scales_dealt")
+        nc.vector.tensor_copy(key_scales_dealt[:], key_scales_picked[:].rearrange("p (m t) -> p t m", t=PACK))
+        dealt_words_view = key_scales_dealt[:].rearrange("p t m -> p (t m)").bitcast(I32)
+        for q in range(4):
+            nc.scalar.dma_start(
+                key_scales[:].bitcast(I32)[32 * q : 32 * q + 4, :],
+                dealt_words_view[32 * q : 32 * q + 32 : 8, :],
+            )
+
+        def pick(table, lst, dtype, name, over=None):
+            picked = sb([P, S], dtype, name, over)
+            nc.vector.tensor_copy(picked[:], table[:].indirect(lst[:]))
+            return picked
+
+        a_words = pick(x_word_table, offs_l, U32, "a_words")
+        a_scales = pick(x_scale_table, offs_l, U8, "a_scales")
+        key_words_picked = pick(d_word_table, k1_l, U32, "key_words_picked")
+        key_words = sb([P, S], U32, "key_words")
+        nc.vector.tensor_copy(
+            key_words[:].rearrange("p (t m) -> p m t", t=PACK),
+            key_words_picked[:].rearrange("p (m t) -> p m t", t=PACK),
+        )
+
+        def scores(words, scales, name):
+            banks = []
+            for t in range(PACK):
+                bank = psum.tile([P, S], F32, name="%s_bank%d" % (name, t), tag="%s_bank%d" % (name, t))
+                cols = slice(t * P, (t + 1) * P)
+                nc.tensor.matmul_mx(
+                    out=bank[:], lhsT=key_words[:, cols].bitcast(FP8X4), lhsT_scale=key_scales[:, cols],
+                    rhs=words[:].bitcast(FP8X4), rhs_scale=scales[:], start=True, stop=True,
+                )
+                banks.append(bank)
+            return banks
+
+        a_banks = scores(a_words, a_scales, "a")
+        b_words = pick(x_word_table, two_l, U32, "b_words", over="key_words_picked")
+        b_scales = pick(x_scale_table, two_l, U8, "b_scales", over="d_word_table")
+        b_banks = scores(b_words, b_scales, "b")
+        n1_l = load_list(n1, "n1_l")
+        n2_l = load_list(n2, "n2_l")
+        n3_l = load_list(n3, "n3_l")
+        n4_l = load_list(n4, "n4_l")
+
+        gn_t = sb([P, PACK], F32, "gn_t")
+        nc.gpsimd.dma_start(gn_t[:], gn.rearrange("(p t) o -> p (t o)", t=PACK))
+        gm_t = sb([P, PACK], F32, "gm_t")
+        nc.gpsimd.dma_start(gm_t[:], gm.rearrange("(p t) o -> p (t o)", t=PACK))
+        gn_half = sb([P, PACK], F32, "gn_half")
+        nc.gpsimd.tensor_scalar(gn_half[:], gn_t[:], 0.5, 0.0, ALU.mult, ALU.add)
+        gm_scaled = sb([P, PACK], F32, "gm_scaled")
+        nc.gpsimd.tensor_scalar(gm_scaled[:], gm_t[:], SCORE_SCALE, 0.0, ALU.mult, ALU.add)
+        w_raw = [sb([P, S], U32, "w_raw%d" % i) for i in range(2)]
+        for i, (words, scales) in enumerate(((w1_words, w1_scales), (w2_words, w2_scales))):
+            nc.sync.dma_start(w_raw[i][:].bitcast(I32), words_of(words))
+            for q in range(4):
+                nc.gpsimd.dma_start(
+                    w_scale_raw[:].bitcast(I32)[32 * q + 4 * i : 32 * q + 4 * i + 4, :],
+                    scales[0].bitcast(I32)[4 * q : 4 * q + 4, :],
+                )
+        n5_l = load_list(n5, "n5_l")
+        n6_l = load_list(n6, "n6_l")
+        n7_l = load_list(n7, "n7_l")
+
+        a_last = sb([P, S], F32, "a_last")
+        a_plain = [a_win[t + 1][:, S:] for t in range(PACK - 1)] + [a_last[:]]
+        for t in range(PACK):
+            nc.scalar.activation(a_win[t][:, :S], a_banks[t][:], ACT.Copy, scale=SCORE_SCALE)
+            if t < 2:
+                nc.scalar.activation(a_plain[t], a_banks[t][:], ACT.Copy, scale=SCORE_SCALE)
+            else:
+                nc.sync.dma_start(a_plain[t], a_win[t][:, :S])
+
+        below = sb([P, PACK, S], F32, "below")
+        above = sb([P, PACK, S], F32, "above")
+        below_g = sb([P, PACK, S], F32, "below_g")
+        above_g = sb([P, PACK, S], F32, "above_g")
+        b_win = [sb([P, S], F32, "b_win%d" % t) for t in range(PACK)]
+        b_fetched = sb([P, PACK, S], F32, "b_fetched")
+        st_win = [sb([P, S], F32, "st_win%d" % t) for t in range(PACK)]
+
+        def step_a(t):
+            nc.vector.tensor_tensor(below[:, t, :], a_win[t][:].indirect(n1_l[:]), a_plain[t], ALU.subtract)
+            nc.vector.tensor_tensor(above[:, t, :], a_win[t][:].indirect(n2_l[:]), a_plain[t], ALU.subtract)
+            nc.vector.tensor_scalar(below_g[:, t, :], below[:, t, :], 0.0, gn_t[:, t : t + 1], ALU.min, ALU.mult)
+            nc.vector.tensor_scalar(above_g[:, t, :], above[:, t, :], 0.0, gn_half[:, t : t + 1], ALU.max, ALU.mult)
+
+        b_gained = sb([P, PACK, S], F32, "b_gained")
+
+        def fetch_b(t):
+            nc.scalar.activation(b_win[t][:], b_banks[t][:], ACT.Copy, scale=SCORE_SCALE)
+            nc.scalar.activation(b_gained[:, t, :], b_banks[t][:], ACT.Copy, scale=gm_scaled[:, t : t + 1])
+            for lo, hi in HALVES:
+                nc.scalar.activation(b_fetched[:, t, lo:hi], b_win[t][:].indirect(entries(n3_l, lo, hi)), ACT.Copy)
+
+        def step_b(t):
+            nc.vector.tensor_tensor(st_win[t][:], b_fetched[:, t, :], b_win[t][:], ALU.subtract)
+
+        for t in range(PACK):
+            step_a(t)
+            fetch_b(t)
+            if t > 0:
+                step_b(t - 1)
+        step_b(PACK - 1)
+
+        w_words = [sb([P, S], U32, "w_words%d" % i, over="a_win%d" % i) for i in range(2)]
+        for i in range(2):
+            nc.vector.tensor_copy(
+                w_words[i][:].rearrange("p (t m) -> p m t", t=PACK),
+                w_raw[i][:].rearrange("p (m t) -> p m t", t=PACK),
+            )
+        w_scales = sb([P, S], U8, "w_scales", over="a_win2")
+        nc.vector.tensor_copy(
+            w_scales[:].rearrange("p (t m) -> p t m", t=PACK),
+            w_scale_raw[:].rearrange("p (m t) -> p t m", t=PACK),
+        )
+
+        gate = sb([P, PACK, S], F32, "gate")
+        for lo, hi in HALVES:
+            for t in range(PACK):
+                nc.scalar.activation(gate[:, t, lo:hi], st_win[t][:].indirect(entries(n4_l, lo, hi)), ACT.Sigmoid)
+
+        z_bf = sb([P, S, PACK], BF16, "z_bf")
+        nc.vector.tensor_tensor(line_walk_words(z_bf[:]), line_walk_rows(above_g[:]), line_walk_rows(below_g[:]), ALU.subtract)
+        z_words = sb([P, S], U32, "z_words")
+        z_scales = sb([P, S], U8, "z_scales")
+        z2_bf = sb([P, S, PACK], BF16, "z2_bf")
+        z2_words = sb([P, S], U32, "z2_words")
+        z2_scales = sb([P, S], U8, "z2_scales")
+
+        def gate_z2(lo, hi):
+            nc.vector.tensor_tensor(
+                line_walk_words(z2_bf[:, lo:hi, :]), line_walk_rows(b_gained[:, :, lo:hi]), line_walk_rows(gate[:, :, lo:hi]), ALU.mult
+            )
+
+        def quantise(words, scales, rounded, lo, hi):
+            nc.vector.quantize_mx(
+                out=words[:, lo:hi].bitcast(FP8X4), scales=scales[:, lo:hi],
+                in_=rounded[:, lo:hi, :].rearrange("p j t -> p (j t)"),
+            )
+
+        gate_z2(*HALVES[0])
+        quantise(z_words, z_scales, z_bf, 0, S)
+        quantise(z2_words, z2_scales, z2_bf, *HALVES[0])
+        gate_z2(*HALVES[1])
+        quantise(z2_words, z2_scales, z2_bf, *HALVES[1])
+
+        h = sb([P, PACK, S], F32, "h")
+        for half, (lo, hi) in enumerate(HALVES):
+            banks = []
+            for t in range(PACK):
+                tag = "%s_bank%d" % ("ab"[half], t)
+                bank = psum.tile([P, hi - lo], F32, name="h_" + tag, tag=tag)
+                banks.append(bank)
+            for i, (words, scales) in enumerate(((z_words, z_scales), (z2_words, z2_scales))):
+                for t in range(PACK):
+                    cols = slice(t * P, (t + 1) * P)
+                    nc.tensor.matmul_mx(
+                        out=banks[t][:], lhsT=w_words[i][:, cols].bitcast(FP8X4), lhsT_scale=w_scales[4 * i :, cols],
+                        rhs=words[:, lo:hi].bitcast(FP8X4), rhs_scale=scales[:, lo:hi], start=(i == 0), stop=(i == 1),
+                    )
+            for t in range(PACK):
+                if half == 1 and t % 2 == 1:
+                    nc.vector.tensor_copy(h[:, t, lo:hi], banks[t][:])
+                else:
+                    nc.scalar.copy(h[:, t, lo:hi], banks[t][:])
+
+        h5 = sb([P, PACK, S], F32, "h5")
+        h6 = sb([P, PACK, S], F32, "h6")
+        h7 = sb([P, PACK, S], F32, "h7")
+        first = sb([P, PACK, S], F32, "first")
+        second = sb([P, PACK, S], F32, "second")
+        result = sb([P, PACK, S], F32, "result")
+        out_bf = sb([P, S, PACK], BF16, "out_bf")
+        out_words = sb([P, S], U32, "out_words")
+        out_scales = sb([P, S], U8, "out_scales")
+        out_rows = out_0.rearrange("(p t) j -> p t j", t=PACK)
+
+        def fetch_on_scalar(dst, lst, lo, hi):
+            for t in range(PACK):
+                nc.scalar.activation(dst[:, t, lo:hi], h[:, t, :].indirect(entries(lst, lo, hi)), ACT.Copy)
+
+        def fetch_on_vector(dst, lst, lo, hi, tiles):
+            for t in tiles:
+                nc.vector.tensor_copy(dst[:, t, lo:hi], h[:, t, :].indirect(entries(lst, lo, hi)))
+
+        def larger_first(lo, hi):
+            nc.vector.tensor_tensor(first[:, :, lo:hi], h[:, :, lo:hi], h5[:, :, lo:hi], ALU.max)
+
+        def larger_second(lo, hi):
+            nc.vector.tensor_tensor(second[:, :, lo:hi], h6[:, :, lo:hi], h7[:, :, lo:hi], ALU.max)
+
+        def subtract(lo, hi):
+            nc.vector.tensor_tensor(result[:, :, lo:hi], first[:, :, lo:hi], second[:, :, lo:hi], ALU.subtract)
+            nc.sync.dma_start(out_rows[:, :, lo:hi], result[:, :, lo:hi])
+
+        def round_out(lo, hi):
+            nc.vector.tensor_copy(line_walk_words(out_bf[:, lo:hi, :]), line_walk_rows(result[:, :, lo:hi]))
+
+        def quantise_out(lo, hi):
+            quantise(out_words, out_scales, out_bf, lo, hi)
+            nc.sync.dma_start(words_of(out_1)[:, lo:hi], out_words[:, lo:hi].bitcast(I32))
+
+        c0, c1, c2 = OUT_CHUNKS
+        fetch_on_vector(h7, n7_l, *c0, (1, 0, 3, 2))
+        fetch_on_scalar(h5, n5_l, *c0)
+        fetch_on_vector(h7, n7_l, *c1, (0,))
+        larger_first(*c0)
+        fetch_on_scalar(h6, n6_l, *c0)
+        fetch_on_vector(h7, n7_l, *c1, (1, 2, 3))
+        fetch_on_scalar(h5, n5_l, *c1)
+        fetch_on_scalar(h6, n6_l, *c1)
+        fetch_on_scalar(h5, n5_l, *c2)
+        fetch_on_scalar(h6, n6_l, *c2)
+        fetch_on_scalar(h7, n7_l, *c2)
+        larger_second(*c0)
+        larger_first(*c1)
+        subtract(*c0)
+        larger_second(*c1)
+        round_out(*c0)
+        subtract(*c1)
+        quantise_out(*c0)
+        larger_first(*c2)
+        round_out(*c1)
+        larger_second(*c2)
+        quantise_out(*c1)
+        subtract(*c2)
+        round_out(*c2)
+        quantise_out(*c2)
+        for q in range(4):
+            queue = nc.scalar if q % 2 == 0 else nc.sync
+            queue.dma_start(
+                out_2[0].bitcast(I32)[4 * q : 4 * q + 4, :],
+                out_scales[:].bitcast(I32)[32 * q : 32 * q + 4, :],
+            )

@@ -66,14 +66,14 @@ def tile_picked_kjhingehopdmix_none_po_kernel(
         x_word_table = sb([P, T], U32, "x_word_table")
         nc.sync.dma_start(x_word_table[:].bitcast(I32), words_of(x_words))
         offs_l = load_list(offs, "offs_l")
+        d_word_table = sb([P, G], U32, "d_word_table")
+        nc.sync.dma_start(d_word_table[:].bitcast(I32), words_of(d_words))
         x_scale_table = sb([P, T], U8, "x_scale_table")
         for q in range(4):
-            nc.sync.dma_start(
+            nc.scalar.dma_start(
                 x_scale_table[:].bitcast(I32)[32 * q : 32 * q + 32, :],
                 x_scales[0].bitcast(I32)[4 * q : 4 * q + 4, :].unsqueeze(0).to_broadcast([8, 4, T // 4]),
             )
-        d_word_table = sb([P, G], U32, "d_word_table")
-        nc.sync.dma_start(d_word_table[:].bitcast(I32), words_of(d_words))
         two_l = load_list(two, "two_l")
         key_scales = sb([P, S], U8, "key_scales")
         nc.gpsimd.memset(key_scales[:].bitcast(I32), 0)
@@ -82,6 +82,8 @@ def tile_picked_kjhingehopdmix_none_po_kernel(
         a_win = [sb([P, 2 * S], F32, "a_win%d" % t) for t in range(PACK)]
         nc.gpsimd.memset(a_win[0][:, S:], 0.0)
 
+        warm = sb([P, 1], F32, "warm")
+        nc.scalar.activation(warm[:], a_win[0][:, S : S + 1], ACT.Sigmoid)
         key_scales_picked = sb([P, S], U8, "key_scales_picked")
         nc.vector.tensor_copy(key_scales_picked[:], d_scale_table[:].indirect(k1_l[:]))
         key_scales_dealt = sb([P, PACK, P], U8, "key_scales_dealt")
@@ -157,32 +159,38 @@ def tile_picked_kjhingehopdmix_none_po_kernel(
             else:
                 nc.sync.dma_start(a_plain[t], a_win[t][:, :S])
 
-        below = sb([P, PACK, S], F32, "below")
-        above = sb([P, PACK, S], F32, "above")
         below_g = sb([P, PACK, S], F32, "below_g")
         above_g = sb([P, PACK, S], F32, "above_g")
-        b_win = [sb([P, S], F32, "b_win%d" % t) for t in range(PACK)]
+        b_win = [sb([P, 2 * S], F32, "b_win%d" % t) for t in range(PACK)]
+        late = sb([P, PACK, S], F32, "late")
+        below = [b_win[0][:, S:], b_win[2][:, S:], late[:, 0, :], late[:, 2, :]]
+        above = [b_win[1][:, S:], b_win[3][:, S:], late[:, 1, :], late[:, 3, :]]
         b_fetched = sb([P, PACK, S], F32, "b_fetched")
         st_win = [sb([P, S], F32, "st_win%d" % t) for t in range(PACK)]
 
         def step_a(t):
-            nc.vector.tensor_tensor(below[:, t, :], a_win[t][:].indirect(n1_l[:]), a_plain[t], ALU.subtract)
-            nc.vector.tensor_tensor(above[:, t, :], a_win[t][:].indirect(n2_l[:]), a_plain[t], ALU.subtract)
-            nc.vector.tensor_scalar(below_g[:, t, :], below[:, t, :], 0.0, gn_t[:, t : t + 1], ALU.min, ALU.mult)
-            nc.vector.tensor_scalar(above_g[:, t, :], above[:, t, :], 0.0, gn_half[:, t : t + 1], ALU.max, ALU.mult)
+            nc.vector.tensor_tensor(below[t], a_win[t][:].indirect(n1_l[:]), a_plain[t], ALU.subtract)
+            if t < PACK - 1:
+                nc.vector.tensor_tensor(above[t], a_win[t][:].indirect(n2_l[:]), a_plain[t], ALU.subtract)
+            else:
+                nc.vector.tensor_tensor(above[t], a_fetched[:], a_plain[t], ALU.subtract)
+            nc.vector.tensor_scalar(below_g[:, t, :], below[t], 0.0, gn_t[:, t : t + 1], ALU.min, ALU.mult)
+            nc.vector.tensor_scalar(above_g[:, t, :], above[t], 0.0, gn_half[:, t : t + 1], ALU.max, ALU.mult)
 
         b_gained = sb([P, PACK, S], F32, "b_gained")
 
         def fetch_b(t):
-            nc.scalar.activation(b_win[t][:], b_banks[t][:], ACT.Copy, scale=SCORE_SCALE)
+            nc.scalar.activation(b_win[t][:, :S], b_banks[t][:], ACT.Copy, scale=SCORE_SCALE)
             nc.scalar.activation(b_gained[:, t, :], b_banks[t][:], ACT.Copy, scale=gm_scaled[:, t : t + 1])
-            for lo, hi in HALVES:
-                nc.scalar.activation(b_fetched[:, t, lo:hi], b_win[t][:].indirect(entries(n3_l, lo, hi)), ACT.Copy)
+            nc.scalar.activation(b_fetched[:, t, :], b_win[t][:].indirect(n3_l[:]), ACT.Copy)
 
         def step_b(t):
-            nc.vector.tensor_tensor(st_win[t][:], b_fetched[:, t, :], b_win[t][:], ALU.subtract)
+            nc.vector.tensor_tensor(st_win[t][:], b_fetched[:, t, :], b_win[t][:, :S], ALU.subtract)
 
+        a_fetched = sb([P, S], F32, "a_fetched")
         for t in range(PACK):
+            if t == PACK - 2:
+                nc.scalar.activation(a_fetched[:], a_win[PACK - 1][:].indirect(n2_l[:]), ACT.Copy)
             step_a(t)
             fetch_b(t)
             if t > 0:
@@ -280,39 +288,35 @@ def tile_picked_kjhingehopdmix_none_po_kernel(
             nc.vector.tensor_tensor(result[:, :, lo:hi], first[:, :, lo:hi], second[:, :, lo:hi], ALU.subtract)
             nc.sync.dma_start(out_rows[:, :, lo:hi], result[:, :, lo:hi])
 
-        def round_out(lo, hi):
-            nc.vector.tensor_copy(line_walk_words(out_bf[:, lo:hi, :]), line_walk_rows(result[:, :, lo:hi]))
+        def round_out(copy, lo, hi):
+            copy(line_walk_words(out_bf[:, lo:hi, :]), line_walk_rows(result[:, :, lo:hi]))
 
-        def quantise_out(lo, hi):
+        def quantise_out(queue, lo, hi):
             quantise(out_words, out_scales, out_bf, lo, hi)
-            nc.sync.dma_start(words_of(out_1)[:, lo:hi], out_words[:, lo:hi].bitcast(I32))
+            queue.dma_start(words_of(out_1)[:, lo:hi], out_words[:, lo:hi].bitcast(I32))
 
         c0, c1, c2 = OUT_CHUNKS
-        fetch_on_vector(h7, n7_l, *c0, (1, 0, 3, 2))
-        fetch_on_scalar(h5, n5_l, *c0)
-        fetch_on_vector(h7, n7_l, *c1, (0,))
-        larger_first(*c0)
+        fetch_on_vector(h7, n7_l, *HALVES[0], (1, 0, 3, 2))
+        fetch_on_scalar(h5, n5_l, *HALVES[0])
+        fetch_on_vector(h7, n7_l, *HALVES[1], (0,))
+        larger_first(*HALVES[0])
         fetch_on_scalar(h6, n6_l, *c0)
-        fetch_on_vector(h7, n7_l, *c1, (1, 2, 3))
-        fetch_on_scalar(h5, n5_l, *c1)
+        fetch_on_vector(h7, n7_l, *HALVES[1], (1, 2, 3))
+        fetch_on_scalar(h5, n5_l, *HALVES[1])
         fetch_on_scalar(h6, n6_l, *c1)
-        fetch_on_scalar(h5, n5_l, *c2)
         fetch_on_scalar(h6, n6_l, *c2)
-        fetch_on_scalar(h7, n7_l, *c2)
         larger_second(*c0)
-        larger_first(*c1)
         subtract(*c0)
+        larger_first(*HALVES[1])
         larger_second(*c1)
-        round_out(*c0)
+        round_out(nc.scalar.copy, *c0)
         subtract(*c1)
-        quantise_out(*c0)
-        larger_first(*c2)
-        round_out(*c1)
         larger_second(*c2)
-        quantise_out(*c1)
+        round_out(nc.scalar.copy, *c1)
         subtract(*c2)
-        round_out(*c2)
-        quantise_out(*c2)
+        quantise_out(nc.scalar, *HALVES[0])
+        round_out(nc.vector.tensor_copy, *c2)
+        quantise_out(nc.sync, *HALVES[1])
         for q in range(4):
             queue = nc.scalar if q % 2 == 0 else nc.sync
             queue.dma_start(

@@ -32,11 +32,11 @@ def entries(lst, lo, hi):
 
 
 def line_walk_rows(ap):
-    return ap.rearrange("p t (c i) -> p c t i", i=4)
+    return ap.rearrange("p t (c i) -> p c t i", i=2)
 
 
 def line_walk_words(ap):
-    return ap.rearrange("p (c i) t -> p c t i", i=4)
+    return ap.rearrange("p (c i) t -> p c t i", i=2)
 
 
 def tile_picked_kjhingehopdmix_none_po_kernel(

@@ -77,8 +77,6 @@ def tile_picked_kjhingehopdmix_none_po_kernel(
         two_l = load_list(two, "two_l")
         key_scales = sb([P, S], U8, "key_scales")
         nc.gpsimd.memset(key_scales[:].bitcast(I32), 0)
-        w_scale_raw = sb([P, S], U8, "w_scale_raw")
-        nc.gpsimd.memset(w_scale_raw[:].bitcast(I32), 0)
         a_win = [sb([P, 2 * S], F32, "a_win%d" % t) for t in range(PACK)]
         nc.gpsimd.memset(a_win[0][:, S:], 0.0)
 
@@ -127,25 +125,17 @@ def tile_picked_kjhingehopdmix_none_po_kernel(
         b_banks = scores(b_words, b_scales, "b")
         n1_l = load_list(n1, "n1_l")
         n2_l = load_list(n2, "n2_l")
-        n3_l = load_list(n3, "n3_l")
-        n4_l = load_list(n4, "n4_l")
 
         gn_t = sb([P, PACK], F32, "gn_t")
-        nc.gpsimd.dma_start(gn_t[:], gn.rearrange("(p t) o -> p (t o)", t=PACK))
+        nc.sync.dma_start(gn_t[:], gn.rearrange("(p t) o -> p (t o)", t=PACK))
         gm_t = sb([P, PACK], F32, "gm_t")
-        nc.gpsimd.dma_start(gm_t[:], gm.rearrange("(p t) o -> p (t o)", t=PACK))
+        nc.sync.dma_start(gm_t[:], gm.rearrange("(p t) o -> p (t o)", t=PACK))
         gn_half = sb([P, PACK], F32, "gn_half")
-        nc.gpsimd.tensor_scalar(gn_half[:], gn_t[:], 0.5, 0.0, ALU.mult, ALU.add)
+        nc.scalar.activation(gn_half[:], gn_t[:], ACT.Copy, scale=0.5)
         gm_scaled = sb([P, PACK], F32, "gm_scaled")
-        nc.gpsimd.tensor_scalar(gm_scaled[:], gm_t[:], SCORE_SCALE, 0.0, ALU.mult, ALU.add)
-        w_raw = [sb([P, S], U32, "w_raw%d" % i) for i in range(2)]
-        for i, (words, scales) in enumerate(((w1_words, w1_scales), (w2_words, w2_scales))):
-            nc.sync.dma_start(w_raw[i][:].bitcast(I32), words_of(words))
-            for q in range(4):
-                nc.gpsimd.dma_start(
-                    w_scale_raw[:].bitcast(I32)[32 * q + 4 * i : 32 * q + 4 * i + 4, :],
-                    scales[0].bitcast(I32)[4 * q : 4 * q + 4, :],
-                )
+        nc.scalar.activation(gm_scaled[:], gm_t[:], ACT.Copy, scale=SCORE_SCALE)
+        n3_l = load_list(n3, "n3_l")
+        n4_l = load_list(n4, "n4_l")
         n5_l = load_list(n5, "n5_l")
         n6_l = load_list(n6, "n6_l")
         n7_l = load_list(n7, "n7_l")
@@ -162,15 +152,17 @@ def tile_picked_kjhingehopdmix_none_po_kernel(
         below_g = sb([P, PACK, S], F32, "below_g")
         above_g = sb([P, PACK, S], F32, "above_g")
         b_win = [sb([P, 2 * S], F32, "b_win%d" % t) for t in range(PACK)]
-        late = sb([P, PACK, S], F32, "late")
-        below = [b_win[0][:, S:], b_win[2][:, S:], late[:, 0, :], late[:, 2, :]]
-        above = [b_win[1][:, S:], b_win[3][:, S:], late[:, 1, :], late[:, 3, :]]
-        b_fetched = sb([P, PACK, S], F32, "b_fetched")
-        st_win = [sb([P, S], F32, "st_win%d" % t) for t in range(PACK)]
+        late = sb([P, 2, S], F32, "late")
+        below = [b_win[0][:, S:], b_win[2][:, S:]]
+        above = [b_win[1][:, S:], b_win[3][:, S:], late[:, 0, :], late[:, 1, :]]
+        b_fetched = [sb([P, S], F32, "b_fetched%d" % t) for t in range(PACK)]
+        st_win = []
 
         def step_a(t):
+            if t >= 2:
+                below.append(sb([P, S], F32, "below%d" % t, over="b_fetched%d" % (t - 2))[:])
             nc.vector.tensor_tensor(below[t], a_win[t][:].indirect(n1_l[:]), a_plain[t], ALU.subtract)
-            if t < PACK - 1:
+            if t != PACK - 2:
                 nc.vector.tensor_tensor(above[t], a_win[t][:].indirect(n2_l[:]), a_plain[t], ALU.subtract)
             else:
                 nc.vector.tensor_tensor(above[t], a_fetched[:], a_plain[t], ALU.subtract)
@@ -182,28 +174,40 @@ def tile_picked_kjhingehopdmix_none_po_kernel(
         def fetch_b(t):
             nc.scalar.activation(b_win[t][:, :S], b_banks[t][:], ACT.Copy, scale=SCORE_SCALE)
             nc.scalar.activation(b_gained[:, t, :], b_banks[t][:], ACT.Copy, scale=gm_scaled[:, t : t + 1])
-            nc.scalar.activation(b_fetched[:, t, :], b_win[t][:].indirect(n3_l[:]), ACT.Copy)
+            nc.scalar.activation(b_fetched[t][:], b_win[t][:].indirect(n3_l[:]), ACT.Copy)
 
         def step_b(t):
-            nc.vector.tensor_tensor(st_win[t][:], b_fetched[:, t, :], b_win[t][:, :S], ALU.subtract)
+            st_win.append(sb([P, S], F32, "st_win%d" % t, over=("a_win1", "a_win2", "a_win3", "a_last")[t]))
+            nc.vector.tensor_tensor(st_win[t][:], b_fetched[t][:], b_win[t][:, :S], ALU.subtract)
 
         a_fetched = sb([P, S], F32, "a_fetched")
         for t in range(PACK):
             if t == PACK - 2:
-                nc.scalar.activation(a_fetched[:], a_win[PACK - 1][:].indirect(n2_l[:]), ACT.Copy)
+                nc.scalar.activation(a_fetched[:], a_win[t][:].indirect(n2_l[:]), ACT.Copy)
             step_a(t)
-            fetch_b(t)
             if t > 0:
+                fetch_b(t - 1)
                 step_b(t - 1)
+        fetch_b(PACK - 1)
         step_b(PACK - 1)
 
-        w_words = [sb([P, S], U32, "w_words%d" % i, over="a_win%d" % i) for i in range(2)]
+        w_scale_raw = sb([P, S], U8, "w_scale_raw", over="key_words")
+        nc.gpsimd.memset(w_scale_raw[:].bitcast(I32), 0)
+        w_raw = sb([P, 2, S], U32, "w_raw", over="a_win0")
+        for i, (words, scales) in enumerate(((w1_words, w1_scales), (w2_words, w2_scales))):
+            nc.sync.dma_start(w_raw[:, i, :].bitcast(I32), words_of(words))
+            for q in range(4):
+                nc.sync.dma_start(
+                    w_scale_raw[:].bitcast(I32)[32 * q + 4 * i : 32 * q + 4 * i + 4, :],
+                    scales[0].bitcast(I32)[4 * q : 4 * q + 4, :],
+                )
+        w_words = [sb([P, S], U32, "w_words%d" % i, over=("b_win2", "b_fetched2")[i]) for i in range(2)]
         for i in range(2):
             nc.vector.tensor_copy(
                 w_words[i][:].rearrange("p (t m) -> p m t", t=PACK),
-                w_raw[i][:].rearrange("p (m t) -> p m t", t=PACK),
+                w_raw[:, i, :].rearrange("p (m t) -> p m t", t=PACK),
             )
-        w_scales = sb([P, S], U8, "w_scales", over="a_win2")
+        w_scales = sb([P, S], U8, "w_scales", over="b_fetched3")
         nc.vector.tensor_copy(
             w_scales[:].rearrange("p (t m) -> p t m", t=PACK),
             w_scale_raw[:].rearrange("p (m t) -> p t m", t=PACK),
@@ -214,11 +218,11 @@ def tile_picked_kjhingehopdmix_none_po_kernel(
             for t in range(PACK):
                 nc.scalar.activation(gate[:, t, lo:hi], st_win[t][:].indirect(entries(n4_l, lo, hi)), ACT.Sigmoid)
 
-        z_bf = sb([P, S, PACK], BF16, "z_bf")
+        z_bf = sb([P, S, PACK], BF16, "z_bf", over="b_win3")
         nc.vector.tensor_tensor(line_walk_words(z_bf[:]), line_walk_rows(above_g[:]), line_walk_rows(below_g[:]), ALU.subtract)
         z_words = sb([P, S], U32, "z_words")
         z_scales = sb([P, S], U8, "z_scales")
-        z2_bf = sb([P, S, PACK], BF16, "z2_bf")
+        z2_bf = sb([P, S, PACK], BF16, "z2_bf", over="below_g")
         z2_words = sb([P, S], U32, "z2_words")
         z2_scales = sb([P, S], U8, "z2_scales")
 

@@ -207,16 +207,16 @@ def tile_picked_kjhingehopdmix_none_po_kernel(
                 w_words[i][:].rearrange("p (t m) -> p m t", t=PACK),
                 w_raw[:, i, :].rearrange("p (m t) -> p m t", t=PACK),
             )
-        w_scales = sb([P, S], U8, "w_scales", over="b_fetched3")
+        w_scales = sb([P, S], U8, "w_scales", over="late")
         nc.vector.tensor_copy(
             w_scales[:].rearrange("p (t m) -> p t m", t=PACK),
             w_scale_raw[:].rearrange("p (m t) -> p t m", t=PACK),
         )
 
-        gate = sb([P, PACK, S], F32, "gate")
+        gate = {0: sb([P, PACK, S // 2], F32, "gate0"), S // 2: sb([P, PACK, S // 2], F32, "gate1", over="b_fetched3")}
         for lo, hi in HALVES:
             for t in range(PACK):
-                nc.scalar.activation(gate[:, t, lo:hi], st_win[t][:].indirect(entries(n4_l, lo, hi)), ACT.Sigmoid)
+                nc.scalar.activation(gate[lo][:, t, :], st_win[t][:].indirect(entries(n4_l, lo, hi)), ACT.Sigmoid)
 
         z_bf = sb([P, S, PACK], BF16, "z_bf", over="b_win3")
         nc.vector.tensor_tensor(line_walk_words(z_bf[:]), line_walk_rows(above_g[:]), line_walk_rows(below_g[:]), ALU.subtract)
@@ -228,7 +228,7 @@ def tile_picked_kjhingehopdmix_none_po_kernel(
 
         def gate_z2(lo, hi):
             nc.vector.tensor_tensor(
-                line_walk_words(z2_bf[:, lo:hi, :]), line_walk_rows(b_gained[:, :, lo:hi]), line_walk_rows(gate[:, :, lo:hi]), ALU.mult
+                line_walk_words(z2_bf[:, lo:hi, :]), line_walk_rows(b_gained[:, :, lo:hi]), line_walk_rows(gate[lo][:]), ALU.mult
             )
 
         def quantise(words, scales, rounded, lo, hi):
@@ -313,13 +313,13 @@ def tile_picked_kjhingehopdmix_none_po_kernel(
         subtract(*c0)
         larger_first(*HALVES[1])
         larger_second(*c1)
-        round_out(nc.scalar.copy, *c0)
+        nc.scalar.copy(out_bf[:, c0[0] : c0[1], :], result[:, :, c0[0] : c0[1]].rearrange("p t j -> p j t"))
         subtract(*c1)
         larger_second(*c2)
-        round_out(nc.scalar.copy, *c1)
+        round_out(nc.vector.tensor_copy, *c1)
         subtract(*c2)
-        quantise_out(nc.scalar, *HALVES[0])
         round_out(nc.vector.tensor_copy, *c2)
+        quantise_out(nc.scalar, *HALVES[0])
         quantise_out(nc.sync, *HALVES[1])
         for q in range(4):
             queue = nc.scalar if q % 2 == 0 else nc.sync

from contextlib import ExitStack

import concourse.mybir as mybir

F32 = mybir.dt.float32
BF16 = mybir.dt.bfloat16
I32 = mybir.dt.int32
U32 = mybir.dt.uint32
U16 = mybir.dt.uint16
U8 = mybir.dt.uint8
FP8X4 = mybir.dt.float8_e4m3fn_x4
ALU = mybir.AluOpType
ACT = mybir.ActivationFunctionType

P = 128
PACK = 4
S = 512
T = 1024
G = 2048
SCORE_SCALE = 0.0625
FLOPS = 4 * 2 * 512 * 512 * 512
HALVES = [(0, 256), (256, 512)]
OUT_CHUNKS = [(0, 256), (256, 384), (384, 512)]


def words_of(dram):
    return dram[0].rearrange("p n t -> p (n t)").bitcast(I32)


def entries(lst, lo, hi):
    return lst[:, lo // 16 : hi // 16]


def line_walk_rows(ap):
    return ap.rearrange("p t (c i) -> p c t i", i=2)


def line_walk_words(ap):
    return ap.rearrange("p (c i) t -> p c t i", i=2)


def tile_picked_kjhingehopdmix_none_po_kernel(
    tc, x_words, x_scales, d_words, d_scales, gn, gm, w1_words, w1_scales, w2_words, w2_scales,
    offs, k1, two, n1, n2, n3, n4, n5, n6, n7, out_0, out_1, out_2,
):
    nc = tc.nc
    with ExitStack() as ctx:
        lists = ctx.enter_context(tc.tile_pool(name="lists", bufs=1))
        keep = ctx.enter_context(tc.tile_pool(name="keep", bufs=1))
        psum = ctx.enter_context(tc.psum_pool(name="psum", bufs=1))

        def load_list(dram, name):
            lst = lists.tile([P, S // 16], U16, name=name)
            nc.sync.dma_start(lst[:], dram)
            return lst

        def sb(shape, dtype, name, over=None):
            return keep.tile(shape, dtype, name=name, tag=over or name, align_bytes=64)

        k1_l = load_list(k1, "k1_l")
        d_scale_table = sb([P, G], U8, "d_scale_table")
        nc.sync.dma_start(
            d_scale_table[:].bitcast(I32),
            d_scales[0].bitcast(I32).unsqueeze(1).to_broadcast([16, 8, G // 4]),
        )
        x_word_table = sb([P, T], U32, "x_word_table")
        nc.sync.dma_start(x_word_table[:].bitcast(I32), words_of(x_words))
        offs_l = load_list(offs, "offs_l")
        d_word_table = sb([P, G], U32, "d_word_table")
        nc.sync.dma_start(d_word_table[:].bitcast(I32), words_of(d_words))
        x_scale_table = sb([P, T], U8, "x_scale_table")
        for q in range(4):
            nc.scalar.dma_start(
                x_scale_table[:].bitcast(I32)[32 * q : 32 * q + 32, :],
                x_scales[0].bitcast(I32)[4 * q : 4 * q + 4, :].unsqueeze(0).to_broadcast([8, 4, T // 4]),
            )
        two_l = load_list(two, "two_l")
        key_scales = sb([P, S], U8, "key_scales")
        nc.gpsimd.memset(key_scales[:].bitcast(I32), 0)
        a_win = [sb([P, 2 * S], F32, "a_win%d" % t) for t in range(PACK)]
        nc.gpsimd.memset(a_win[0][:, S:], 0.0)

        warm = sb([P, 1], F32, "warm")
        nc.scalar.activation(warm[:], a_win[0][:, S : S + 1], ACT.Sigmoid)
        key_scales_picked = sb([P, S], U8, "key_scales_picked")
        nc.vector.tensor_copy(key_scales_picked[:], d_scale_table[:].indirect(k1_l[:]))
        key_scales_dealt = sb([P, PACK, P], U8, "key_scales_dealt")
        nc.vector.tensor_copy(key_scales_dealt[:], key_scales_picked[:].rearrange("p (m t) -> p t m", t=PACK))
        dealt_words_view = key_scales_dealt[:].rearrange("p t m -> p (t m)").bitcast(I32)
        for q in range(4):
            nc.scalar.dma_start(
                key_scales[:].bitcast(I32)[32 * q : 32 * q + 4, :],
                dealt_words_view[32 * q : 32 * q + 32 : 8, :],
            )

        def pick(table, lst, dtype, name, over=None):
            picked = sb([P, S], dtype, name, over)
            nc.vector.tensor_copy(picked[:], table[:].indirect(lst[:]))
            return picked

        a_words = pick(x_word_table, offs_l, U32, "a_words")
        a_scales = pick(x_scale_table, offs_l, U8, "a_scales")
        key_words_picked = pick(d_word_table, k1_l, U32, "key_words_picked")
        key_words = sb([P, S], U32, "key_words")
        nc.vector.tensor_copy(
            key_words[:].rearrange("p (t m) -> p m t", t=PACK),
            key_words_picked[:].rearrange("p (m t) -> p m t", t=PACK),
        )

        def scores(words, scales, name):
            banks = []
            for t in range(PACK):
                bank = psum.tile([P, S], F32, name="%s_bank%d" % (name, t), tag="%s_bank%d" % (name, t))
                cols = slice(t * P, (t + 1) * P)
                nc.tensor.matmul_mx(
                    out=bank[:], lhsT=key_words[:, cols].bitcast(FP8X4), lhsT_scale=key_scales[:, cols],
                    rhs=words[:].bitcast(FP8X4), rhs_scale=scales[:], start=True, stop=True,
                )
                banks.append(bank)
            return banks

        a_banks = scores(a_words, a_scales, "a")
        b_words = pick(x_word_table, two_l, U32, "b_words", over="key_words_picked")
        b_scales = pick(x_scale_table, two_l, U8, "b_scales", over="d_word_table")
        b_banks = scores(b_words, b_scales, "b")
        n1_l = load_list(n1, "n1_l")
        n2_l = load_list(n2, "n2_l")

        gn_t = sb([P, PACK], F32, "gn_t")
        nc.sync.dma_start(gn_t[:], gn.rearrange("(p t) o -> p (t o)", t=PACK))
        gm_t = sb([P, PACK], F32, "gm_t")
        nc.sync.dma_start(gm_t[:], gm.rearrange("(p t) o -> p (t o)", t=PACK))
        gn_half = sb([P, PACK], F32, "gn_half")
        nc.scalar.activation(gn_half[:], gn_t[:], ACT.Copy, scale=0.5)
        gm_scaled = sb([P, PACK], F32, "gm_scaled")
        nc.scalar.activation(gm_scaled[:], gm_t[:], ACT.Copy, scale=SCORE_SCALE)
        n3_l = load_list(n3, "n3_l")
        n4_l = load_list(n4, "n4_l")
        n5_l = load_list(n5, "n5_l")
        n6_l = load_list(n6, "n6_l")
        n7_l = load_list(n7, "n7_l")

        a_last = sb([P, S], F32, "a_last")
        a_plain = [a_win[t + 1][:, S:] for t in range(PACK - 1)] + [a_last[:]]
        for t in range(PACK):
            nc.scalar.activation(a_win[t][:, :S], a_banks[t][:], ACT.Copy, scale=SCORE_SCALE)
            if t < 2:
                nc.scalar.activation(a_plain[t], a_banks[t][:], ACT.Copy, scale=SCORE_SCALE)
            else:
                nc.sync.dma_start(a_plain[t], a_win[t][:, :S])

        below_g = sb([P, PACK, S], F32, "below_g")
        above_g = sb([P, PACK, S], F32, "above_g")
        b_win = [sb([P, 2 * S], F32, "b_win%d" % t) for t in range(PACK)]
        late = sb([P, 2, S], F32, "late")
        below = [b_win[0][:, S:], b_win[2][:, S:]]
        above = [b_win[1][:, S:], b_win[3][:, S:], late[:, 0, :], late[:, 1, :]]
        b_fetched = [sb([P, S], F32, "b_fetched%d" % t) for t in range(PACK)]
        st_win = []

        def step_a(t):
            if t >= 2:
                below.append(sb([P, S], F32, "below%d" % t, over="b_fetched%d" % (t - 2))[:])
            nc.vector.tensor_tensor(below[t], a_win[t][:].indirect(n1_l[:]), a_plain[t], ALU.subtract)
            if t != PACK - 2:
                nc.vector.tensor_tensor(above[t], a_win[t][:].indirect(n2_l[:]), a_plain[t], ALU.subtract)
            else:
                nc.vector.tensor_tensor(above[t], a_fetched[:], a_plain[t], ALU.subtract)
            nc.vector.tensor_scalar(below_g[:, t, :], below[t], 0.0, gn_t[:, t : t + 1], ALU.min, ALU.mult)
            nc.vector.tensor_scalar(above_g[:, t, :], above[t], 0.0, gn_half[:, t : t + 1], ALU.max, ALU.mult)

        b_gained = sb([P, PACK, S], F32, "b_gained")

        def fetch_b(t):
            nc.scalar.activation(b_win[t][:, :S], b_banks[t][:], ACT.Copy, scale=SCORE_SCALE)
            nc.scalar.activation(b_gained[:, t, :], b_banks[t][:], ACT.Copy, scale=gm_scaled[:, t : t + 1])
            nc.scalar.activation(b_fetched[t][:], b_win[t][:].indirect(n3_l[:]), ACT.Copy)

        def step_b(t):
            st_win.append(sb([P, S], F32, "st_win%d" % t, over=("a_win1", "a_win2", "a_win3", "a_last")[t]))
            nc.vector.tensor_tensor(st_win[t][:], b_fetched[t][:], b_win[t][:, :S], ALU.subtract)

        a_fetched = sb([P, S], F32, "a_fetched")
        for t in range(PACK):
            if t == PACK - 2:
                nc.scalar.activation(a_fetched[:], a_win[t][:].indirect(n2_l[:]), ACT.Copy)
            step_a(t)
            if t > 0:
                fetch_b(t - 1)
                step_b(t - 1)
        fetch_b(PACK - 1)
        step_b(PACK - 1)

        w_scale_raw = sb([P, S], U8, "w_scale_raw", over="key_words")
        nc.gpsimd.memset(w_scale_raw[:].bitcast(I32), 0)
        w_raw = sb([P, 2, S], U32, "w_raw", over="a_win0")
        for i, (words, scales) in enumerate(((w1_words, w1_scales), (w2_words, w2_scales))):
            nc.sync.dma_start(w_raw[:, i, :].bitcast(I32), words_of(words))
            for q in range(4):
                nc.sync.dma_start(
                    w_scale_raw[:].bitcast(I32)[32 * q + 4 * i : 32 * q + 4 * i + 4, :],
                    scales[0].bitcast(I32)[4 * q : 4 * q + 4, :],
                )
        w_words = [sb([P, S], U32, "w_words%d" % i, over=("b_win2", "b_fetched2")[i]) for i in range(2)]
        for i in range(2):
            nc.vector.tensor_copy(
                w_words[i][:].rearrange("p (t m) -> p m t", t=PACK),
                w_raw[:, i, :].rearrange("p (m t) -> p m t", t=PACK),
            )
        w_scales = sb([P, S], U8, "w_scales", over="late")
        nc.vector.tensor_copy(
            w_scales[:].rearrange("p (t m) -> p t m", t=PACK),
            w_scale_raw[:].rearrange("p (m t) -> p t m", t=PACK),
        )

        gate = {0: sb([P, PACK, S // 2], F32, "gate0"), S // 2: sb([P, PACK, S // 2], F32, "gate1", over="b_fetched3")}
        for lo, hi in HALVES:
            for t in range(PACK):
                nc.scalar.activation(gate[lo][:, t, :], st_win[t][:].indirect(entries(n4_l, lo, hi)), ACT.Sigmoid)

        z_bf = sb([P, S, PACK], BF16, "z_bf", over="b_win3")
        nc.vector.tensor_tensor(line_walk_words(z_bf[:]), line_walk_rows(above_g[:]), line_walk_rows(below_g[:]), ALU.subtract)
        z_words = sb([P, S], U32, "z_words")
        z_scales = sb([P, S], U8, "z_scales")
        z2_bf = sb([P, S, PACK], BF16, "z2_bf", over="below_g")
        z2_words = sb([P, S], U32, "z2_words")
        z2_scales = sb([P, S], U8, "z2_scales")

        def gate_z2(lo, hi):
            nc.vector.tensor_tensor(
                line_walk_words(z2_bf[:, lo:hi, :]), line_walk_rows(b_gained[:, :, lo:hi]), line_walk_rows(gate[lo][:]), ALU.mult
            )

        def quantise(words, scales, rounded, lo, hi):
            nc.vector.quantize_mx(
                out=words[:, lo:hi].bitcast(FP8X4), scales=scales[:, lo:hi],
                in_=rounded[:, lo:hi, :].rearrange("p j t -> p (j t)"),
            )

        gate_z2(*HALVES[0])
        quantise(z_words, z_scales, z_bf, 0, S)
        quantise(z2_words, z2_scales, z2_bf, *HALVES[0])
        gate_z2(*HALVES[1])
        quantise(z2_words, z2_scales, z2_bf, *HALVES[1])

        h = sb([P, PACK, S], F32, "h")
        for half, (lo, hi) in enumerate(HALVES):
            banks = []
            for t in range(PACK):
                tag = "%s_bank%d" % ("ab"[half], t)
                bank = psum.tile([P, hi - lo], F32, name="h_" + tag, tag=tag)
                banks.append(bank)
            for i, (words, scales) in enumerate(((z_words, z_scales), (z2_words, z2_scales))):
                for t in range(PACK):
                    cols = slice(t * P, (t + 1) * P)
                    nc.tensor.matmul_mx(
                        out=banks[t][:], lhsT=w_words[i][:, cols].bitcast(FP8X4), lhsT_scale=w_scales[4 * i :, cols],
                        rhs=words[:, lo:hi].bitcast(FP8X4), rhs_scale=scales[:, lo:hi], start=(i == 0), stop=(i == 1),
                    )
            for t in range(PACK):
                if half == 1 and t % 2 == 1:
                    nc.vector.tensor_copy(h[:, t, lo:hi], banks[t][:])
                else:
                    nc.scalar.copy(h[:, t, lo:hi], banks[t][:])

        h5 = sb([P, PACK, S], F32, "h5")
        h6 = sb([P, PACK, S], F32, "h6")
        h7 = sb([P, PACK, S], F32, "h7")
        first = sb([P, PACK, S], F32, "first")
        second = sb([P, PACK, S], F32, "second")
        result = sb([P, PACK, S], F32, "result")
        out_bf = sb([P, S, PACK], BF16, "out_bf")
        out_words = sb([P, S], U32, "out_words")
        out_scales = sb([P, S], U8, "out_scales")
        out_rows = out_0.rearrange("(p t) j -> p t j", t=PACK)

        def fetch_on_scalar(dst, lst, lo, hi):
            for t in range(PACK):
                nc.scalar.activation(dst[:, t, lo:hi], h[:, t, :].indirect(entries(lst, lo, hi)), ACT.Copy)

        def fetch_on_vector(dst, lst, lo, hi, tiles):
            for t in tiles:
                nc.vector.tensor_copy(dst[:, t, lo:hi], h[:, t, :].indirect(entries(lst, lo, hi)))

        def larger_first(lo, hi):
            nc.vector.tensor_tensor(first[:, :, lo:hi], h[:, :, lo:hi], h5[:, :, lo:hi], ALU.max)

        def larger_second(lo, hi):
            nc.vector.tensor_tensor(second[:, :, lo:hi], h6[:, :, lo:hi], h7[:, :, lo:hi], ALU.max)

        def subtract(lo, hi):
            nc.vector.tensor_tensor(result[:, :, lo:hi], first[:, :, lo:hi], second[:, :, lo:hi], ALU.subtract)
            nc.sync.dma_start(out_rows[:, :, lo:hi], result[:, :, lo:hi])

        def round_out(copy, lo, hi):
            copy(line_walk_words(out_bf[:, lo:hi, :]), line_walk_rows(result[:, :, lo:hi]))

        def quantise_out(queue, lo, hi):
            quantise(out_words, out_scales, out_bf, lo, hi)
            queue.dma_start(words_of(out_1)[:, lo:hi], out_words[:, lo:hi].bitcast(I32))

        c0, c1, c2 = OUT_CHUNKS
        fetch_on_vector(h7, n7_l, *HALVES[0], (1, 0, 3, 2))
        fetch_on_scalar(h5, n5_l, *HALVES[0])
        fetch_on_vector(h7, n7_l, *HALVES[1], (0,))
        larger_first(*HALVES[0])
        fetch_on_scalar(h6, n6_l, *c0)
        fetch_on_vector(h7, n7_l, *HALVES[1], (1, 2, 3))
        fetch_on_scalar(h5, n5_l, *HALVES[1])
        fetch_on_scalar(h6, n6_l, *c1)
        fetch_on_scalar(h6, n6_l, *c2)
        larger_second(*c0)
        subtract(*c0)
        larger_first(*HALVES[1])
        larger_second(*c1)
        nc.scalar.copy(out_bf[:, c0[0] : c0[1], :], result[:, :, c0[0] : c0[1]].rearrange("p t j -> p j t"))
        subtract(*c1)
        larger_second(*c2)
        round_out(nc.vector.tensor_copy, *c1)
        subtract(*c2)
        round_out(nc.vector.tensor_copy, *c2)
        quantise_out(nc.scalar, *HALVES[0])
        quantise_out(nc.sync, *HALVES[1])
        for q in range(4):
            queue = nc.scalar if q % 2 == 0 else nc.sync
            queue.dma_start(
                out_2[0].bitcast(I32)[4 * q : 4 * q + 4, :],
                out_scales[:].bitcast(I32)[32 * q : 32 * q + 4, :],
            )
